import numpy as np
import ml_dtypes


def mxq(x, axis, fmt="e4m3"):
    dtype, down = {"e4m3": (ml_dtypes.float8_e4m3fn, 7), "e5m2": (ml_dtypes.float8_e5m2, 14)}[fmt]
    v = np.moveaxis(np.asarray(x, np.float32).astype(ml_dtypes.bfloat16).astype(np.float64), axis, -1)
    blocks = v.reshape(v.shape[:-1] + (-1, 32))
    amax = np.abs(blocks).max(-1, keepdims=True)
    byte = np.maximum(np.where(amax > 0, np.frexp(amax)[1] - 1 + 127, 0) - down, 1)
    scale = np.exp2(byte - 127.0)
    codes = (blocks / scale).astype(np.float32).astype(dtype).astype(np.float64)
    return np.moveaxis((codes * scale).reshape(v.shape), -1, axis)


WIDE = False


def mx_kscale(k):
    if not WIDE:
        return np.ones(k)
    levels = np.array([10, -10, 5, -5, 0])
    if k % 512:
        return np.exp2(np.random.permutation(np.resize(levels, k // 32))).repeat(32)
    a = np.empty((k // 512, 16))
    for p in range(k // 512):
        a[p, :8] = np.random.permutation(np.resize(levels, 8))
        for g in range(8):
            far = levels[np.abs(levels - a[p, g]) >= 10]
            a[p, g + 8] = far[np.random.randint(len(far))]
    return np.exp2(a.ravel()).repeat(32)


def f64(x):
    return np.asarray(x).astype(np.float64)


def striped(idx):
    return np.tile(idx.reshape(-1, 16).T, (8, 1)).astype(np.uint16)


def unstriped(offs):
    return offs[:16].T.reshape(-1).astype(np.int64)


E2M1 = np.array([0.0, 0.5, 1.0, 1.5, 2.0, 3.0, 4.0, 6.0, -0.0, -0.5, -1.0, -1.5, -2.0, -3.0, -4.0, -6.0])


def pack_weight(w, fmt):
    k, n = w.shape
    w = f64(np.asarray(w, np.float32).astype(ml_dtypes.bfloat16)).reshape(k // 32, 32, n)
    amax = np.abs(w).max(1)
    if fmt == "e4m3":
        byte = np.frexp(amax)[1] - 1 + 127 - 7
    else:
        mant, ex = np.frexp(amax / 6.0)
        byte = np.where(mant > 0.5, ex, ex - 1) + 127
    byte = np.clip(np.where(amax > 0, byte, 1), 1, 254)
    scaled = (w * np.exp2(127.0 - byte)[:, None, :]).reshape(k, n).astype(np.float32)
    by_word = np.ascontiguousarray(scaled.reshape(k // 512, 128, 4, n).transpose(0, 1, 3, 2))
    if fmt == "e4m3":
        words = by_word.astype(ml_dtypes.float8_e4m3fn).view(np.uint8)
    else:
        c = by_word.astype(ml_dtypes.float4_e2m1fn).view(np.uint8) & 0xF
        words = (c[..., 0::2] | (c[..., 1::2] << 4)).reshape(k // 512, 128, 2 * n)
    return np.ascontiguousarray(words), np.ascontiguousarray(byte.astype(np.uint8).reshape(k // 512, 16, n))


def unpack_weight(words, scales, fmt):
    g, _, n = scales.shape
    words = np.ascontiguousarray(words).reshape(g, 128, n, -1)
    if fmt == "e4m3":
        vals = words.view(ml_dtypes.float8_e4m3fn).astype(np.float64)
    else:
        nib = np.empty((g, 128, n, 4), np.uint8)
        nib[..., 0::2] = words & 0xF
        nib[..., 1::2] = words >> 4
        vals = E2M1[nib]
    vals = vals * np.repeat(np.exp2(scales.astype(np.float64) - 127.0), 8, axis=1)[..., None]
    return vals.transpose(0, 1, 3, 2).reshape(g * 512, n)


def silu(v):
    return v / (1.0 + np.exp(-np.maximum(v, -700.0)))


def d_silu(v):
    s = 1.0 / (1.0 + np.exp(-np.maximum(v, -700.0)))
    return s * (1.0 + v * (1.0 - s))


K, T, E, C, H, N = 256, 1024, 8, 256, 512, 512


def by_expert(wq, xq):
    return np.concatenate([wq[e].T @ xq[:, e * C:(e + 1) * C] for e in range(E)], axis=1)


def setup_inputs():
    n = np.random.standard_normal
    s = mx_kscale(N)[:, None]
    u = mx_kscale(H)
    first = np.random.permutation(np.repeat(np.arange(E), T // E))
    second = (first + 1 + np.random.permutation(np.repeat(np.arange(E - 1), -(-T // (E - 1)))[:T])) % E
    while np.bincount(second, minlength=E).max() != T // E:
        load = np.bincount(second, minlength=E); hi, lo = int(load.argmax()), int(load.argmin())
        t = np.flatnonzero((second == hi) & (first != lo))[0]; second[t] = lo
    slot_token = np.empty(E * C, np.int64); pos = np.empty((2, T), np.int64); fill = np.zeros(E, np.int64)
    place = np.stack([np.random.permutation(C) for _ in range(E)])
    for r, deal in enumerate((first, second)):
        for t in np.random.permutation(T):
            e = deal[t]; j = e * C + place[e, fill[e]]; fill[e] += 1; slot_token[j] = t; pos[r, t] = j
    g = np.random.uniform(0.2, 0.8, T)
    w_slot = np.empty(E * C); w_slot[pos[0]] = g; w_slot[pos[1]] = 1.0 - g
    w2 = [pack_weight(m, "e2m1") for m in n((E, N, H)) / np.sqrt(N) / s[None] * u[None, None, :]]
    w1 = [pack_weight(m, "e2m1") for m in n((E, H, K)) / np.sqrt(H) / u[None, :, None]]
    w3 = [pack_weight(m, "e2m1") for m in n((E, H, K)) / np.sqrt(H) / u[None, :, None]]
    return {
        "dyT": (n((N, T)) * s).astype(np.float32),
        "a1": n((H, E * C)).astype(np.float32),
        "a3": n((H, E * C)).astype(np.float32),
        "w2_words": np.stack([m[0] for m in w2]),
        "w2_scales": np.stack([m[1] for m in w2]),
        "w1_words": np.stack([m[0] for m in w1]),
        "w1_scales": np.stack([m[1] for m in w1]),
        "w3_words": np.stack([m[0] for m in w3]),
        "w3_scales": np.stack([m[1] for m in w3]),
        "gate": np.tile(w_slot, (N, 1)).astype(np.float32),
        "offs": striped(slot_token),
        "pos1": striped(pos[0]),
        "pos2": striped(pos[1]),
    }


def reference(dyT, a1, a3, w2_words, w2_scales, w1_words, w1_scales, w3_words, w3_scales, gate, offs, pos1, pos2):
    idx = unstriped(offs)
    w2 = np.stack([unpack_weight(w2_words[e], w2_scales[e], "e2m1") for e in range(E)])
    w1 = np.stack([unpack_weight(w1_words[e], w1_scales[e], "e2m1") for e in range(E)])
    w3 = np.stack([unpack_weight(w3_words[e], w3_scales[e], "e2m1") for e in range(E)])
    gq = mxq(f64(gate) * f64(dyT)[:, idx], 0, "e4m3")
    dh = by_expert(w2, gq)
    da1 = dh * f64(a3) * d_silu(f64(a1))
    da3 = dh * silu(f64(a1))
    dx = by_expert(w1, mxq(da1, 0, "e4m3")) + by_expert(w3, mxq(da3, 0, "e4m3"))
    return dx[:, unstriped(pos1)] + dx[:, unstriped(pos2)]

@@ -1,0 +1,231 @@
+from contextlib import ExitStack
+
+import concourse.mybir as mybir
+
+K, T, E, C, H, N = 256, 1024, 8, 256, 512, 512
+S = E * C
+FLOPS = 2 * S * N * H + 2 * (2 * S * H * K)
+BYTES = 4 * (N * T + 2 * H * S + S + K * T) + E * (2 * 128 * H + 16 * H + 2 * (2 * 128 * K + 16 * K)) + 2 * 128 * (S + 2 * T) // 16
+
+F32 = mybir.dt.float32
+BF16 = mybir.dt.bfloat16
+U32 = mybir.dt.uint32
+I32 = mybir.dt.int32
+U16 = mybir.dt.uint16
+U8 = mybir.dt.uint8
+FP8X4 = mybir.dt.float8_e4m3fn_x4
+FP4X4 = mybir.dt.float4_e2m1fn_x4
+ADD, SUB, MULT = mybir.AluOpType.add, mybir.AluOpType.subtract, mybir.AluOpType.mult
+IDENT = mybir.ActivationFunctionType.Identity
+SILU = mybir.ActivationFunctionType.Silu
+TANH = mybir.ActivationFunctionType.Tanh
+
+P = 128
+CH = 512
+NCH = S // CH
+EPC = CH // C
+
+
+def tile_moe_bdx_glu_silu_kernel(
+    tc, dyT, a1, a3, w2_words, w2_scales, w1_words, w1_scales, w3_words, w3_scales, gate, offs, pos1, pos2, out
+):
+    nc = tc.nc
+    with ExitStack() as ctx:
+        lists = ctx.enter_context(tc.tile_pool(name="lists", bufs=1))
+        keep = ctx.enter_context(tc.tile_pool(name="keep", bufs=1))
+        raw = ctx.enter_context(tc.tile_pool(name="raw", bufs=2))
+        acts = ctx.enter_context(tc.tile_pool(name="acts", bufs=2))
+        grad = ctx.enter_context(tc.tile_pool(name="grad", bufs=3))
+        deriv = ctx.enter_context(tc.tile_pool(name="deriv", bufs=2))
+        fin = ctx.enter_context(tc.tile_pool(name="fin", bufs=2))
+        psum_h = ctx.enter_context(tc.psum_pool(name="psum_h", bufs=5))
+        psum_x = ctx.enter_context(tc.psum_pool(name="psum_x", bufs=3))
+
+        offs_t = lists.tile([P, S // 16], U16, name="offs_t")
+        pos1_t = lists.tile([P, T // 16], U16, name="pos1_t")
+        pos2_t = lists.tile([P, T // 16], U16, name="pos2_t")
+        dy = [keep.tile([P, T], F32, name=f"dy{t}") for t in range(4)]
+        gates = [keep.tile([P, CH], F32, name=f"gates{c}") for c in range(NCH)]
+        w2_sraw = keep.tile([P, E, H], U8, name="w2_sraw", align_bytes=64)
+        w2 = keep.tile([P, E, 2 * H], U8, name="w2", align_bytes=64)
+        w2_s = keep.tile([P, E, H], U8, name="w2_s", align_bytes=64)
+        w1 = keep.tile([P, E, 2 * K], U8, name="w1", align_bytes=64)
+        w1_s = keep.tile([P, E, K], U8, name="w1_s", align_bytes=64)
+        w3 = keep.tile([P, E, 2 * K], U8, name="w3", align_bytes=64)
+        w3_s = keep.tile([P, E, K], U8, name="w3_s", align_bytes=64)
+        dx = [keep.tile([P, S], F32, name=f"dx{k}") for k in range(2)]
+
+        half = keep.tile([P, 1], F32, name="half")
+        nc.gpsimd.memset(half[:], -0.5)
+        nc.gpsimd.memset(w2_sraw[:].bitcast(I32), 0)
+        nc.gpsimd.memset(w1_s[:].bitcast(I32), 0)
+        nc.gpsimd.memset(w3_s[:].bitcast(I32), 0)
+
+        def load_scales(plane, scales):
+            rows = scales.bitcast(I32).rearrange("e s f i -> f (e s) i")
+            for q in range(4):
+                nc.sync.dma_start(plane[32 * q : 32 * q + 4, :, :].bitcast(I32), rows[4 * q : 4 * q + 4])
+
+        dy_rows = dyT.rearrange("(p t) n -> p t n", t=4)
+        a1_rows = a1.rearrange("(p r) s -> p r s", r=4)
+        a3_rows = a3.rearrange("(p r) s -> p r s", r=4)
+
+        w2_raw, a1_t, a3_t = {}, {}, {}
+
+        def load_w2(c):
+            es = slice(c * EPC, (c + 1) * EPC)
+            w2_c = raw.tile([P, EPC, 2 * H], U8, name="w2_c", align_bytes=64)
+            nc.sync.dma_start(w2_c[:].bitcast(I32), w2_words.bitcast(I32).rearrange("e s p b -> p (e s) b")[:, es, :])
+            w2_raw[c] = w2_c
+
+        def load_gate(c):
+            nc.sync.dma_start(gates[c][:], gate[0:P, c * CH : (c + 1) * CH])
+
+        def load_acts(c):
+            cols = slice(c * CH, (c + 1) * CH)
+            a1_c = acts.tile([P, 4, CH], F32, name="a1_c")
+            a3_c = acts.tile([P, 4, CH], F32, name="a3_c")
+            nc.sync.dma_start(a1_c[:], a1_rows[:, :, cols])
+            nc.sync.dma_start(a3_c[:], a3_rows[:, :, cols])
+            a1_t[c], a3_t[c] = a1_c, a3_c
+
+        nc.sync.dma_start(offs_t[:], offs)
+        nc.sync.dma_start(dy[0][:], dy_rows[:, 0, :])
+        load_gate(0)
+        for t in range(1, 4):
+            nc.sync.dma_start(dy[t][:], dy_rows[:, t, :])
+        load_gate(1)
+        load_w2(0)
+        load_acts(0)
+        load_scales(w2_sraw, w2_scales)
+        load_gate(2)
+        load_gate(3)
+        nc.sync.dma_start(w1[:].bitcast(I32), w1_words.bitcast(I32).rearrange("e s p b -> p (e s) b"))
+        nc.sync.dma_start(w3[:].bitcast(I32), w3_words.bitcast(I32).rearrange("e s p b -> p (e s) b"))
+        load_scales(w1_s, w1_scales)
+        load_scales(w3_s, w3_scales)
+        load_w2(1)
+        load_acts(1)
+
+        def permute_w2(c):
+            es = slice(c * EPC, (c + 1) * EPC)
+            nc.vector.tensor_copy(
+                out=w2[:, es, :].bitcast(U16).rearrange("p e (r m) -> p e r m", r=4),
+                in_=w2_raw[c][:].bitcast(U16).rearrange("p e (m r) -> p e r m", r=4),
+            )
+            nc.vector.tensor_copy(
+                out=w2_s[:, es, :].rearrange("p e (r m) -> p e r m", r=4),
+                in_=w2_sraw[:, es, :].rearrange("p e (m r) -> p e r m", r=4),
+            )
+
+        def gather(c):
+            g32 = grad.tile([P, 4, CH], F32, name="g32")
+            for t in range(4):
+                nc.vector.tensor_tensor(
+                    g32[:, t, :],
+                    dy[t][:].indirect(offs_t[:, c * CH // 16 : (c + 1) * CH // 16]),
+                    gates[c][:],
+                    MULT,
+                )
+            g16 = grad.tile([P, CH, 4], BF16, name="g16", align_bytes=64)
+            nc.scalar.copy(
+                g16[:].rearrange("p (c i) t -> p c t i", i=4), g32[:].rearrange("p t (c i) -> p c t i", i=4)
+            )
+            return g16
+
+        def quantize_g(g16):
+            gq = grad.tile([P, CH], U32, name="gq", align_bytes=64)
+            gs = grad.tile([P, CH], U8, name="gs", align_bytes=64)
+            nc.vector.quantize_mx(
+                out=gq[:].bitcast(FP8X4), scales=gs[:], in_=g16[:].rearrange("p n t -> p (n t)")
+            )
+            return gq, gs
+
+        def activations(c):
+            zn = acts.tile([P, 4, CH], F32, name="zn")
+            ms = acts.tile([P, 2, 4, CH], F32, name="ms")
+            for u in range(0, CH, 256):
+                us = slice(u, u + 256)
+                a1_u, zn_u, rn_u = a1_t[c][:, :, us], zn[:, :, us], ms[:, 0, :, us]
+                nc.scalar.activation(zn_u, a1_u, SILU, scale=-1.0)
+                nc.scalar.activation(rn_u, a1_u, TANH, scale=0.5)
+                nc.scalar.activation(rn_u, rn_u, IDENT, scale=-0.5, bias=half[:])
+                nc.scalar.activation(ms[:, 1, :, us], a1_u, SILU)
+                nc.vector.scalar_tensor_tensor(zn_u, zn_u, 1.0, a3_t[c][:, :, us], SUB, MULT)
+                nc.gpsimd.tensor_tensor(rn_u, zn_u, rn_u, MULT)
+            return ms
+
+        def expert(e, gq, gs, ms):
+            base = (e % EPC) * C
+            dd = deriv.tile([P, 2, C, 4], BF16, name="dd", align_bytes=64)
+            for h in range(C // P):
+                cols = slice(base + h * P, base + (h + 1) * P)
+                dh = psum_h.tile([P, 4, P], F32, name="dh")
+                for r in range(4):
+                    nc.tensor.matmul_mx(
+                        out=dh[:, r, :],
+                        lhsT=w2[:, e, r * 2 * P : (r + 1) * 2 * P].bitcast(FP4X4),
+                        lhsT_scale=w2_s[:, e, r * P : (r + 1) * P],
+                        rhs=gq[:, cols].bitcast(FP8X4),
+                        rhs_scale=gs[:, cols],
+                        start=True,
+                        stop=True,
+                    )
+                rows = slice(h * P, (h + 1) * P)
+                nc.vector.tensor_tensor(
+                    dd[:, :, rows, :],
+                    dh[:].rearrange("p r n -> p n r").unsqueeze(1).to_broadcast([P, 2, P, 4]),
+                    ms[:, :, :, cols].rearrange("p x r n -> p x n r"),
+                    MULT,
+                )
+            dq = deriv.tile([P, 2, C], U32, name="dq", align_bytes=64)
+            ds = deriv.tile([P, 2, C], U8, name="ds", align_bytes=64)
+            nc.vector.quantize_mx(
+                out=dq[:].rearrange("p x n -> p (x n)").bitcast(FP8X4),
+                scales=ds[:].rearrange("p x n -> p (x n)"),
+                in_=dd[:].rearrange("p x n r -> p (x n r)"),
+            )
+            acc = psum_x.tile([P, 2, C], F32, name="acc")
+            for k in range(2):
+                for h in range(C // P):
+                    cols = slice(h * P, (h + 1) * P)
+                    for x, w, w_s in ((0, w1, w1_s), (1, w3, w3_s)):
+                        nc.tensor.matmul_mx(
+                            out=acc[:, k, cols],
+                            lhsT=w[:, e, k * 2 * P : (k + 1) * 2 * P].bitcast(FP4X4),
+                            lhsT_scale=w_s[:, e, k * P : (k + 1) * P],
+                            rhs=dq[:, x, cols].bitcast(FP8X4),
+                            rhs_scale=ds[:, x, cols],
+                            start=(x == 0),
+                            stop=(x == 1),
+                        )
+                nc.scalar.copy(dx[k][:, e * C : (e + 1) * C], acc[:, k, :])
+
+        g16 = gather(0)
+        permute_w2(0)
+        for c in range(NCH):
+            gqs = quantize_g(g16)
+            if c + 1 < NCH:
+                g16 = gather(c + 1)
+            ms = activations(c)
+            if c + 2 < NCH:
+                load_w2(c + 2)
+                load_acts(c + 2)
+            if c + 2 == NCH:
+                nc.sync.dma_start(pos1_t[:], pos1)
+                nc.sync.dma_start(pos2_t[:], pos2)
+            for e in range(c * EPC, (c + 1) * EPC):
+                expert(e, gqs[0], gqs[1], ms)
+            if c + 1 < NCH:
+                permute_w2(c + 1)
+
+        for k in range(2):
+            for j0, width in [[0,512],[512,512]]:
+                ent = slice(j0 // 16, (j0 + width) // 16)
+                x1 = fin.tile([P, width], F32, name="x1")
+                x2 = fin.tile([P, width], F32, name="x2")
+                nc.vector.tensor_copy(x1[:], dx[k][:].indirect(pos1_t[:, ent]))
+                nc.vector.tensor_copy(x2[:], dx[k][:].indirect(pos2_t[:, ent]))
+                y = fin.tile([P, width], F32, name="y")
+                nc.gpsimd.tensor_tensor(y[:], x1[:], x2[:], ADD)
+                nc.sync.dma_start(out[k * P : (k + 1) * P, j0 : j0 + width], y[:])

@@ -81,31 +81,41 @@ def tile_moe_bdx_glu_silu_kernel(
         def load_gate(c):
             nc.sync.dma_start(gates[c][:], gate[0:P, c * CH : (c + 1) * CH])
 
-        def load_acts(c):
-            cols = slice(c * CH, (c + 1) * CH)
+        def act_tiles(c):
             a1_c = acts.tile([P, 4, CH], F32, name="a1_c")
             a3_c = acts.tile([P, 4, CH], F32, name="a3_c")
-            nc.sync.dma_start(a1_c[:], a1_rows[:, :, cols])
-            nc.sync.dma_start(a3_c[:], a3_rows[:, :, cols])
             a1_t[c], a3_t[c] = a1_c, a3_c
 
+        def load_act(tile, rows, c, j0, width):
+            nc.sync.dma_start(tile[:, :, j0 : j0 + width], rows[:, :, c * CH + j0 : c * CH + j0 + width])
+
+        def load_acts(c):
+            act_tiles(c)
+            load_act(a1_t[c], a1_rows, c, 0, CH)
+            load_act(a3_t[c], a3_rows, c, 0, CH)
+
+        act_tiles(0)
         nc.sync.dma_start(offs_t[:], offs)
         nc.sync.dma_start(dy[0][:], dy_rows[:, 0, :])
         load_gate(0)
-        for t in range(1, 4):
-            nc.sync.dma_start(dy[t][:], dy_rows[:, t, :])
+        nc.sync.dma_start(dy[1][:], dy_rows[:, 1, :])
+        nc.sync.dma_start(dy[2][:], dy_rows[:, 2, :])
+        load_act(a1_t[0], a1_rows, 0, 0, C)
+        nc.sync.dma_start(dy[3][:], dy_rows[:, 3, :])
+        load_act(a1_t[0], a1_rows, 0, C, C)
         load_gate(1)
         load_w2(0)
-        load_acts(0)
         load_scales(w2_sraw, w2_scales)
+        load_act(a3_t[0], a3_rows, 0, 0, C)
+        load_act(a3_t[0], a3_rows, 0, C, C)
         load_gate(2)
-        load_gate(3)
         nc.sync.dma_start(w1[:].bitcast(I32), w1_words.bitcast(I32).rearrange("e s p b -> p (e s) b"))
         nc.sync.dma_start(w3[:].bitcast(I32), w3_words.bitcast(I32).rearrange("e s p b -> p (e s) b"))
         load_scales(w1_s, w1_scales)
         load_scales(w3_s, w3_scales)
         load_w2(1)
         load_acts(1)
+        load_gate(3)
 
         def permute_w2(c):
             es = slice(c * EPC, (c + 1) * EPC)
@@ -172,12 +182,13 @@ def tile_moe_bdx_glu_silu_kernel(
                         stop=True,
                     )
                 rows = slice(h * P, (h + 1) * P)
-                nc.vector.tensor_tensor(
-                    dd[:, :, rows, :],
-                    dh[:].rearrange("p r n -> p n r").unsqueeze(1).to_broadcast([P, 2, P, 4]),
-                    ms[:, :, :, cols].rearrange("p x r n -> p x n r"),
-                    MULT,
-                )
+                for x in range(2):
+                    nc.vector.tensor_tensor(
+                        dd[:, x, rows, :].rearrange("p (c i) r -> p c r i", i=4),
+                        dh[:].rearrange("p r (c i) -> p c r i", i=4),
+                        ms[:, x, :, cols].rearrange("p r (c i) -> p c r i", i=4),
+                        MULT,
+                    )
             dq = deriv.tile([P, 2, C], U32, name="dq", align_bytes=64)
             ds = deriv.tile([P, 2, C], U8, name="ds", align_bytes=64)
             nc.vector.quantize_mx(
@@ -202,22 +213,25 @@ def tile_moe_bdx_glu_silu_kernel(
                 nc.scalar.copy(dx[k][:, e * C : (e + 1) * C], acc[:, k, :])
 
         g16 = gather(0)
+        ms = activations(0)
         permute_w2(0)
+        gqs = quantize_g(g16)
         for c in range(NCH):
-            gqs = quantize_g(g16)
-            if c + 1 < NCH:
-                g16 = gather(c + 1)
-            ms = activations(c)
             if c + 2 < NCH:
                 load_w2(c + 2)
                 load_acts(c + 2)
             if c + 2 == NCH:
                 nc.sync.dma_start(pos1_t[:], pos1)
                 nc.sync.dma_start(pos2_t[:], pos2)
+            if c + 1 < NCH:
+                g16 = gather(c + 1)
+                next_gqs = quantize_g(g16)
+                permute_w2(c + 1)
             for e in range(c * EPC, (c + 1) * EPC):
                 expert(e, gqs[0], gqs[1], ms)
             if c + 1 < NCH:
-                permute_w2(c + 1)
+                ms = activations(c + 1)
+                gqs = next_gqs
 
         for k in range(2):
             for j0, width in [[0,512],[512,512]]:

@@ -162,7 +162,7 @@ def tile_moe_bdx_glu_silu_kernel(
                 nc.scalar.activation(rn_u, rn_u, IDENT, scale=-0.5, bias=half[:])
                 nc.scalar.activation(ms[:, 1, :, us], a1_u, SILU)
                 nc.vector.scalar_tensor_tensor(zn_u, zn_u, 1.0, a3_t[c][:, :, us], SUB, MULT)
-                nc.gpsimd.tensor_tensor(rn_u, zn_u, rn_u, MULT)
+                nc.vector.tensor_tensor(rn_u, zn_u, rn_u, MULT)
             return ms
 
         def expert(e, gq, gs, ms):
@@ -234,12 +234,12 @@ def tile_moe_bdx_glu_silu_kernel(
                 gqs = next_gqs
 
         for k in range(2):
-            for j0, width in [[0,512],[512,512]]:
+            for j0, width in [[0,512],[512,256],[768,256]]:
                 ent = slice(j0 // 16, (j0 + width) // 16)
                 x1 = fin.tile([P, width], F32, name="x1")
                 x2 = fin.tile([P, width], F32, name="x2")
                 nc.vector.tensor_copy(x1[:], dx[k][:].indirect(pos1_t[:, ent]))
                 nc.vector.tensor_copy(x2[:], dx[k][:].indirect(pos2_t[:, ent]))
                 y = fin.tile([P, width], F32, name="y")
-                nc.gpsimd.tensor_tensor(y[:], x1[:], x2[:], ADD)
+                nc.vector.tensor_tensor(y[:], x1[:], x2[:], ADD)
                 nc.sync.dma_start(out[k * P : (k + 1) * P, j0 : j0 + width], y[:])

@@ -24,6 +24,10 @@ P = 128
 CH = 512
 NCH = S // CH
 EPC = CH // C
+TILE_N = 128
+ON_GPSIMD = (2, 3, 4, 5, 6, 7)
+AHEAD = 2
+LAST_PIECES = ((0, 512), (512, 256), (768, 256))
 
 
 def tile_moe_bdx_glu_silu_kernel(
@@ -31,13 +35,17 @@ def tile_moe_bdx_glu_silu_kernel(
 ):
     nc = tc.nc
     with ExitStack() as ctx:
-        lists = ctx.enter_context(tc.tile_pool(name="lists", bufs=1))
-        keep = ctx.enter_context(tc.tile_pool(name="keep", bufs=1))
-        raw = ctx.enter_context(tc.tile_pool(name="raw", bufs=2))
-        acts = ctx.enter_context(tc.tile_pool(name="acts", bufs=2))
-        grad = ctx.enter_context(tc.tile_pool(name="grad", bufs=3))
-        deriv = ctx.enter_context(tc.tile_pool(name="deriv", bufs=2))
-        fin = ctx.enter_context(tc.tile_pool(name="fin", bufs=2))
+        pool = lambda name, bufs: ctx.enter_context(tc.tile_pool(name=name, bufs=bufs))
+        lists = pool("lists", 1)
+        keep = pool("keep", 1)
+        raw = pool("raw", 2)
+        saved = pool("saved", 2)
+        zpool = pool("zpool", 3)
+        factors = pool("factors", 5)
+        gathered = pool("gathered", 2)
+        grad = pool("grad", 4)
+        deriv = pool("deriv", 2)
+        fin = pool("fin", 2)
         psum_h = ctx.enter_context(tc.psum_pool(name="psum_h", bufs=5))
         psum_x = ctx.enter_context(tc.psum_pool(name="psum_x", bufs=3))
 
@@ -55,11 +63,8 @@ def tile_moe_bdx_glu_silu_kernel(
         w3_s = keep.tile([P, E, K], U8, name="w3_s", align_bytes=64)
         dx = [keep.tile([P, S], F32, name=f"dx{k}") for k in range(2)]
 
-        half = keep.tile([P, 1], F32, name="half")
-        nc.gpsimd.memset(half[:], -0.5)
-        nc.gpsimd.memset(w2_sraw[:].bitcast(I32), 0)
-        nc.gpsimd.memset(w1_s[:].bitcast(I32), 0)
-        nc.gpsimd.memset(w3_s[:].bitcast(I32), 0)
+        for plane in (w2_sraw, w1_s, w3_s):
+            nc.gpsimd.memset(plane[:].bitcast(I32), 0)
 
         def load_scales(plane, scales):
             rows = scales.bitcast(I32).rearrange("e s f i -> f (e s) i")
@@ -69,53 +74,53 @@ def tile_moe_bdx_glu_silu_kernel(
         dy_rows = dyT.rearrange("(p t) n -> p t n", t=4)
         a1_rows = a1.rearrange("(p r) s -> p r s", r=4)
         a3_rows = a3.rearrange("(p r) s -> p r s", r=4)
-
         w2_raw, a1_t, a3_t = {}, {}, {}
 
-        def load_w2(c):
-            es = slice(c * EPC, (c + 1) * EPC)
-            w2_c = raw.tile([P, EPC, 2 * H], U8, name="w2_c", align_bytes=64)
-            nc.sync.dma_start(w2_c[:].bitcast(I32), w2_words.bitcast(I32).rearrange("e s p b -> p (e s) b")[:, es, :])
-            w2_raw[c] = w2_c
+        def load_dy(t):
+            nc.sync.dma_start(dy[t][:], dy_rows[:, t, :])
 
         def load_gate(c):
             nc.sync.dma_start(gates[c][:], gate[0:P, c * CH : (c + 1) * CH])
 
-        def act_tiles(c):
-            a1_c = acts.tile([P, 4, CH], F32, name="a1_c")
-            a3_c = acts.tile([P, 4, CH], F32, name="a3_c")
+        def load_words(tile, words, es):
+            nc.sync.dma_start(tile.bitcast(I32), words.bitcast(I32).rearrange("e s p b -> p (e s) b")[:, es, :])
+
+        def load_w2(c):
+            w2_c = raw.tile([P, EPC, 2 * H], U8, name="w2_c", align_bytes=64)
+            load_words(w2_c[:], w2_words, slice(c * EPC, (c + 1) * EPC))
+            w2_raw[c] = w2_c
+
+        def new_saved(c):
+            a1_c = saved.tile([P, 4, CH], F32, name="a1_c")
+            a3_c = saved.tile([P, 4, CH], F32, name="a3_c")
             a1_t[c], a3_t[c] = a1_c, a3_c
 
-        def load_act(tile, rows, c, j0, width):
+        def load_saved(tile, rows, c, j0=0, width=CH):
             nc.sync.dma_start(tile[:, :, j0 : j0 + width], rows[:, :, c * CH + j0 : c * CH + j0 + width])
 
-        def load_acts(c):
-            act_tiles(c)
-            load_act(a1_t[c], a1_rows, c, 0, CH)
-            load_act(a3_t[c], a3_rows, c, 0, CH)
-
-        act_tiles(0)
+        new_saved(0)
         nc.sync.dma_start(offs_t[:], offs)
-        nc.sync.dma_start(dy[0][:], dy_rows[:, 0, :])
+        load_dy(0)
         load_gate(0)
-        nc.sync.dma_start(dy[1][:], dy_rows[:, 1, :])
-        nc.sync.dma_start(dy[2][:], dy_rows[:, 2, :])
-        load_act(a1_t[0], a1_rows, 0, 0, C)
-        nc.sync.dma_start(dy[3][:], dy_rows[:, 3, :])
-        load_act(a1_t[0], a1_rows, 0, C, C)
+        load_dy(1)
+        load_dy(2)
+        load_saved(a1_t[0], a1_rows, 0, 0, C)
+        load_dy(3)
         load_gate(1)
         load_w2(0)
         load_scales(w2_sraw, w2_scales)
-        load_act(a3_t[0], a3_rows, 0, 0, C)
-        load_act(a3_t[0], a3_rows, 0, C, C)
+        load_saved(a1_t[0], a1_rows, 0, C, C)
         load_gate(2)
-        nc.sync.dma_start(w1[:].bitcast(I32), w1_words.bitcast(I32).rearrange("e s p b -> p (e s) b"))
-        nc.sync.dma_start(w3[:].bitcast(I32), w3_words.bitcast(I32).rearrange("e s p b -> p (e s) b"))
+        load_saved(a3_t[0], a3_rows, 0)
+        load_w2(1)
+        load_gate(3)
+        new_saved(1)
+        load_saved(a1_t[1], a1_rows, 1)
+        load_words(w1[:], w1_words, slice(0, E))
+        load_words(w3[:], w3_words, slice(0, E))
         load_scales(w1_s, w1_scales)
         load_scales(w3_s, w3_scales)
-        load_w2(1)
-        load_acts(1)
-        load_gate(3)
+        load_saved(a3_t[1], a3_rows, 1)
 
         def permute_w2(c):
             es = slice(c * EPC, (c + 1) * EPC)
@@ -128,8 +133,10 @@ def tile_moe_bdx_glu_silu_kernel(
                 in_=w2_sraw[:, es, :].rearrange("p e (m r) -> p e r m", r=4),
             )
 
+        g16, gq, gs = {}, {}, {}
+
         def gather(c):
-            g32 = grad.tile([P, 4, CH], F32, name="g32")
+            g32 = gathered.tile([P, 4, CH], F32, name="g32")
             for t in range(4):
                 nc.vector.tensor_tensor(
                     g32[:, t, :],
@@ -137,109 +144,135 @@ def tile_moe_bdx_glu_silu_kernel(
                     gates[c][:],
                     MULT,
                 )
-            g16 = grad.tile([P, CH, 4], BF16, name="g16", align_bytes=64)
+            g16_c = grad.tile([P, CH, 4], BF16, name="g16_c", align_bytes=64)
             nc.scalar.copy(
-                g16[:].rearrange("p (c i) t -> p c t i", i=4), g32[:].rearrange("p t (c i) -> p c t i", i=4)
+                g16_c[:].rearrange("p (c i) t -> p c t i", i=4), g32[:].rearrange("p t (c i) -> p c t i", i=4)
             )
-            return g16
+            g16[c] = g16_c
 
-        def quantize_g(g16):
-            gq = grad.tile([P, CH], U32, name="gq", align_bytes=64)
-            gs = grad.tile([P, CH], U8, name="gs", align_bytes=64)
+        def quantize_g(c):
+            gq_c = grad.tile([P, CH], U32, name="gq_c", align_bytes=64)
+            gs_c = grad.tile([P, CH], U8, name="gs_c", align_bytes=64)
             nc.vector.quantize_mx(
-                out=gq[:].bitcast(FP8X4), scales=gs[:], in_=g16[:].rearrange("p n t -> p (n t)")
+                out=gq_c[:].bitcast(FP8X4), scales=gs_c[:], in_=g16[c][:].rearrange("p n t -> p (n t)")
             )
-            return gq, gs
+            gq[c], gs[c] = gq_c, gs_c
 
-        def activations(c):
-            zn = acts.tile([P, 4, CH], F32, name="zn")
-            ms = acts.tile([P, 2, 4, CH], F32, name="ms")
-            for u in range(0, CH, 256):
-                us = slice(u, u + 256)
-                a1_u, zn_u, rn_u = a1_t[c][:, :, us], zn[:, :, us], ms[:, 0, :, us]
-                nc.scalar.activation(zn_u, a1_u, SILU, scale=-1.0)
-                nc.scalar.activation(rn_u, a1_u, TANH, scale=0.5)
-                nc.scalar.activation(rn_u, rn_u, IDENT, scale=-0.5, bias=half[:])
-                nc.scalar.activation(ms[:, 1, :, us], a1_u, SILU)
-                nc.vector.scalar_tensor_tensor(zn_u, zn_u, 1.0, a3_t[c][:, :, us], SUB, MULT)
-                nc.vector.tensor_tensor(rn_u, zn_u, rn_u, MULT)
-            return ms
+        ms, zs = {}, {}
 
-        def expert(e, gq, gs, ms):
+        def scalar_part(e):
+            zn = zpool.tile([P, 4, C], F32, name="zn")
+            ms_e = factors.tile([P, 2, 4, C], F32, name="ms_e")
+            mine = a1_t[e // EPC][:, :, (e % EPC) * C : (e % EPC + 1) * C]
+            nc.scalar.activation(zn[:], mine, SILU, scale=-1.0)
+            nc.scalar.activation(ms_e[:, 0], mine, TANH, scale=0.5)
+            nc.scalar.activation(ms_e[:, 0], ms_e[:, 0], IDENT, scale=-0.5, bias=-0.5)
+            nc.scalar.activation(ms_e[:, 1], mine, SILU)
+            ms[e], zs[e] = ms_e, zn
+
+        def times_a3(e):
+            mine = a3_t[e // EPC][:, :, (e % EPC) * C : (e % EPC + 1) * C]
+            nc.vector.scalar_tensor_tensor(zs[e][:], zs[e][:], 1.0, mine, SUB, MULT)
+
+        def times_r(e):
+            engine = nc.gpsimd if e in ON_GPSIMD else nc.vector
+            engine.tensor_tensor(ms[e][:, 0], zs[e][:], ms[e][:, 0], MULT)
+
+        da = {}
+
+        def multiply_dh(e):
             base = (e % EPC) * C
-            dd = deriv.tile([P, 2, C, 4], BF16, name="dd", align_bytes=64)
-            for h in range(C // P):
-                cols = slice(base + h * P, base + (h + 1) * P)
-                dh = psum_h.tile([P, 4, P], F32, name="dh")
+            da_e = deriv.tile([P, 2, 2, TILE_N, 4], BF16, name="da_e", align_bytes=64)
+            for h in range(2):
+                slots = slice(base + h * TILE_N, base + (h + 1) * TILE_N)
+                dh = psum_h.tile([P, 4, TILE_N], F32, name="dh")
                 for r in range(4):
                     nc.tensor.matmul_mx(
                         out=dh[:, r, :],
                         lhsT=w2[:, e, r * 2 * P : (r + 1) * 2 * P].bitcast(FP4X4),
                         lhsT_scale=w2_s[:, e, r * P : (r + 1) * P],
-                        rhs=gq[:, cols].bitcast(FP8X4),
-                        rhs_scale=gs[:, cols],
+                        rhs=gq[e // EPC][:, slots].bitcast(FP8X4),
+                        rhs_scale=gs[e // EPC][:, slots],
                         start=True,
                         stop=True,
                     )
-                rows = slice(h * P, (h + 1) * P)
                 for x in range(2):
                     nc.vector.tensor_tensor(
-                        dd[:, x, rows, :].rearrange("p (c i) r -> p c r i", i=4),
+                        da_e[:, h, x].rearrange("p (c i) r -> p c r i", i=4),
                         dh[:].rearrange("p r (c i) -> p c r i", i=4),
-                        ms[:, x, :, cols].rearrange("p r (c i) -> p c r i", i=4),
+                        ms[e][:, x, :, h * TILE_N : (h + 1) * TILE_N].rearrange("p r (c i) -> p c r i", i=4),
                         MULT,
                     )
-            dq = deriv.tile([P, 2, C], U32, name="dq", align_bytes=64)
-            ds = deriv.tile([P, 2, C], U8, name="ds", align_bytes=64)
-            nc.vector.quantize_mx(
-                out=dq[:].rearrange("p x n -> p (x n)").bitcast(FP8X4),
-                scales=ds[:].rearrange("p x n -> p (x n)"),
-                in_=dd[:].rearrange("p x n r -> p (x n r)"),
-            )
-            acc = psum_x.tile([P, 2, C], F32, name="acc")
-            for k in range(2):
-                for h in range(C // P):
-                    cols = slice(h * P, (h + 1) * P)
-                    for x, w, w_s in ((0, w1, w1_s), (1, w3, w3_s)):
-                        nc.tensor.matmul_mx(
-                            out=acc[:, k, cols],
-                            lhsT=w[:, e, k * 2 * P : (k + 1) * 2 * P].bitcast(FP4X4),
-                            lhsT_scale=w_s[:, e, k * P : (k + 1) * P],
-                            rhs=dq[:, x, cols].bitcast(FP8X4),
-                            rhs_scale=ds[:, x, cols],
-                            start=(x == 0),
-                            stop=(x == 1),
-                        )
-                nc.scalar.copy(dx[k][:, e * C : (e + 1) * C], acc[:, k, :])
+            da[e] = da_e
 
-        g16 = gather(0)
-        ms = activations(0)
-        permute_w2(0)
-        gqs = quantize_g(g16)
+        def finish(e, parts):
+            dq = deriv.tile([P, 2, 2, TILE_N], U32, name="dq", align_bytes=64)
+            ds = deriv.tile([P, 2, 2, TILE_N], U8, name="ds", align_bytes=64)
+            acc = psum_x.tile([P, 2, C], F32, name="acc")
+            per = 2 // parts
+            for part in range(parts):
+                hs = slice(part * per, (part + 1) * per)
+                nc.vector.quantize_mx(
+                    out=dq[:, hs].rearrange("p h x n -> p (h x n)").bitcast(FP8X4),
+                    scales=ds[:, hs].rearrange("p h x n -> p (h x n)"),
+                    in_=da[e][:, hs].rearrange("p h x n r -> p (h x n r)"),
+                )
+                for k in range(2):
+                    for h in range(part * per, (part + 1) * per):
+                        for x, w, w_s in ((0, w1, w1_s), (1, w3, w3_s)):
+                            nc.tensor.matmul_mx(
+                                out=acc[:, k, h * TILE_N : (h + 1) * TILE_N],
+                                lhsT=w[:, e, k * 2 * P : (k + 1) * 2 * P].bitcast(FP4X4),
+                                lhsT_scale=w_s[:, e, k * P : (k + 1) * P],
+                                rhs=dq[:, h, x].bitcast(FP8X4),
+                                rhs_scale=ds[:, h, x],
+                                start=(x == 0),
+                                stop=(x == 1),
+                            )
+                    cols = slice(part * per * TILE_N, (part + 1) * per * TILE_N)
+                    nc.scalar.copy(dx[k][:, e * C + cols.start : e * C + cols.stop], acc[:, k, cols])
+
         for c in range(NCH):
-            if c + 2 < NCH:
-                load_w2(c + 2)
-                load_acts(c + 2)
-            if c + 2 == NCH:
+            gather(c)
+            if c >= 1:
+                quantize_g(c - 1)
+                permute_w2(c - 1)
+                if c + 1 < NCH:
+                    load_w2(c + 1)
+        quantize_g(NCH - 1)
+        permute_w2(NCH - 1)
+
+        for e in range(AHEAD):
+            scalar_part(e)
+        for e in range(AHEAD):
+            times_a3(e)
+        for e in range(AHEAD):
+            times_r(e)
+        for e in range(E):
+            ahead = e + AHEAD
+            if ahead < E:
+                if ahead % EPC == 0 and ahead // EPC + 1 < NCH and ahead // EPC + 1 >= 2:
+                    c = ahead // EPC + 1
+                    new_saved(c)
+                    load_saved(a1_t[c], a1_rows, c)
+                    load_saved(a3_t[c], a3_rows, c)
+                scalar_part(ahead)
+            if e == 3:
                 nc.sync.dma_start(pos1_t[:], pos1)
                 nc.sync.dma_start(pos2_t[:], pos2)
-            if c + 1 < NCH:
-                g16 = gather(c + 1)
-                next_gqs = quantize_g(g16)
-                permute_w2(c + 1)
-            for e in range(c * EPC, (c + 1) * EPC):
-                expert(e, gqs[0], gqs[1], ms)
-            if c + 1 < NCH:
-                ms = activations(c + 1)
-                gqs = next_gqs
+            multiply_dh(e)
+            if ahead < E:
+                times_a3(ahead)
+                times_r(ahead)
+            finish(e, 2 if e == E - 1 else 1)
 
         for k in range(2):
-            for j0, width in [[0,512],[512,256],[768,256]]:
-                ent = slice(j0 // 16, (j0 + width) // 16)
+            for j0, width in LAST_PIECES:
+                entries = slice(j0 // 16, (j0 + width) // 16)
                 x1 = fin.tile([P, width], F32, name="x1")
                 x2 = fin.tile([P, width], F32, name="x2")
-                nc.vector.tensor_copy(x1[:], dx[k][:].indirect(pos1_t[:, ent]))
-                nc.vector.tensor_copy(x2[:], dx[k][:].indirect(pos2_t[:, ent]))
+                nc.vector.tensor_copy(x1[:], dx[k][:].indirect(pos1_t[:, entries]))
+                nc.vector.tensor_copy(x2[:], dx[k][:].indirect(pos2_t[:, entries]))
                 y = fin.tile([P, width], F32, name="y")
                 nc.vector.tensor_tensor(y[:], x1[:], x2[:], ADD)
                 nc.sync.dma_start(out[k * P : (k + 1) * P, j0 : j0 + width], y[:])

@@ -27,7 +27,7 @@ EPC = CH // C
 TILE_N = 128
 ON_GPSIMD = (2, 3, 4, 5, 6, 7)
 AHEAD = 2
-LAST_PIECES = ((0, 512), (512, 256), (768, 256))
+LAST_PIECES = ((0, 512), (512, 512))
 
 
 def tile_moe_bdx_glu_silu_kernel(
@@ -178,13 +178,18 @@ def tile_moe_bdx_glu_silu_kernel(
             engine = nc.gpsimd if e in ON_GPSIMD else nc.vector
             engine.tensor_tensor(ms[e][:, 0], zs[e][:], ms[e][:, 0], MULT)
 
-        da = {}
+        da, da_q, acc = {}, {}, {}
 
-        def multiply_dh(e):
-            base = (e % EPC) * C
+        def new_da(e):
             da_e = deriv.tile([P, 2, 2, TILE_N, 4], BF16, name="da_e", align_bytes=64)
-            for h in range(2):
-                slots = slice(base + h * TILE_N, base + (h + 1) * TILE_N)
+            dq_e = deriv.tile([P, 2, 2, TILE_N], U32, name="dq_e", align_bytes=64)
+            ds_e = deriv.tile([P, 2, 2, TILE_N], U8, name="ds_e", align_bytes=64)
+            acc_e = psum_x.tile([P, 2, C], F32, name="acc_e")
+            da[e], da_q[e], acc[e] = da_e, (dq_e, ds_e), acc_e
+
+        def multiply_dh(e, halves):
+            for h in halves:
+                slots = slice((e % EPC) * C + h * TILE_N, (e % EPC) * C + (h + 1) * TILE_N)
                 dh = psum_h.tile([P, 4, TILE_N], F32, name="dh")
                 for r in range(4):
                     nc.tensor.matmul_mx(
@@ -198,39 +203,34 @@ def tile_moe_bdx_glu_silu_kernel(
                     )
                 for x in range(2):
                     nc.vector.tensor_tensor(
-                        da_e[:, h, x].rearrange("p (c i) r -> p c r i", i=4),
-                        dh[:].rearrange("p r (c i) -> p c r i", i=4),
+                        da[e][:, h, x].rearrange("p (c i) r -> p c r i", i=4),
                         ms[e][:, x, :, h * TILE_N : (h + 1) * TILE_N].rearrange("p r (c i) -> p c r i", i=4),
+                        dh[:].rearrange("p r (c i) -> p c r i", i=4),
                         MULT,
                     )
-            da[e] = da_e
 
-        def finish(e, parts):
-            dq = deriv.tile([P, 2, 2, TILE_N], U32, name="dq", align_bytes=64)
-            ds = deriv.tile([P, 2, 2, TILE_N], U8, name="ds", align_bytes=64)
-            acc = psum_x.tile([P, 2, C], F32, name="acc")
-            per = 2 // parts
-            for part in range(parts):
-                hs = slice(part * per, (part + 1) * per)
-                nc.vector.quantize_mx(
-                    out=dq[:, hs].rearrange("p h x n -> p (h x n)").bitcast(FP8X4),
-                    scales=ds[:, hs].rearrange("p h x n -> p (h x n)"),
-                    in_=da[e][:, hs].rearrange("p h x n r -> p (h x n r)"),
-                )
-                for k in range(2):
-                    for h in range(part * per, (part + 1) * per):
-                        for x, w, w_s in ((0, w1, w1_s), (1, w3, w3_s)):
-                            nc.tensor.matmul_mx(
-                                out=acc[:, k, h * TILE_N : (h + 1) * TILE_N],
-                                lhsT=w[:, e, k * 2 * P : (k + 1) * 2 * P].bitcast(FP4X4),
-                                lhsT_scale=w_s[:, e, k * P : (k + 1) * P],
-                                rhs=dq[:, h, x].bitcast(FP8X4),
-                                rhs_scale=ds[:, h, x],
-                                start=(x == 0),
-                                stop=(x == 1),
-                            )
-                    cols = slice(part * per * TILE_N, (part + 1) * per * TILE_N)
-                    nc.scalar.copy(dx[k][:, e * C + cols.start : e * C + cols.stop], acc[:, k, cols])
+        def finish(e, halves):
+            dq, ds = da_q[e]
+            hs = slice(halves[0], halves[-1] + 1)
+            nc.vector.quantize_mx(
+                out=dq[:, hs].rearrange("p h x n -> p (h x n)").bitcast(FP8X4),
+                scales=ds[:, hs].rearrange("p h x n -> p (h x n)"),
+                in_=da[e][:, hs].rearrange("p h x n r -> p (h x n r)"),
+            )
+            c0, c1 = hs.start * TILE_N, hs.stop * TILE_N
+            for k in range(2):
+                for h in halves:
+                    for x, w, w_s in ((0, w1, w1_s), (1, w3, w3_s)):
+                        nc.tensor.matmul_mx(
+                            out=acc[e][:, k, h * TILE_N : (h + 1) * TILE_N],
+                            lhsT=w[:, e, k * 2 * P : (k + 1) * 2 * P].bitcast(FP4X4),
+                            lhsT_scale=w_s[:, e, k * P : (k + 1) * P],
+                            rhs=dq[:, h, x].bitcast(FP8X4),
+                            rhs_scale=ds[:, h, x],
+                            start=(x == 0),
+                            stop=(x == 1),
+                        )
+                nc.scalar.copy(dx[k][:, e * C + c0 : e * C + c1], acc[e][:, k, c0:c1])
 
         for c in range(NCH):
             gather(c)
@@ -260,19 +260,36 @@ def tile_moe_bdx_glu_silu_kernel(
             if e == 3:
                 nc.sync.dma_start(pos1_t[:], pos1)
                 nc.sync.dma_start(pos2_t[:], pos2)
-            multiply_dh(e)
             if ahead < E:
                 times_a3(ahead)
                 times_r(ahead)
-            finish(e, 2 if e == E - 1 else 1)
+            new_da(e)
+            if e == E - 1:
+                finish(e - 1, (0, 1))
+                for h in range(2):
+                    multiply_dh(e, (h,))
+                    finish(e, (h,))
+            else:
+                multiply_dh(e, (0, 1))
+                if e > 0:
+                    finish(e - 1, (0, 1))
 
-        for k in range(2):
-            for j0, width in LAST_PIECES:
-                entries = slice(j0 // 16, (j0 + width) // 16)
-                x1 = fin.tile([P, width], F32, name="x1")
-                x2 = fin.tile([P, width], F32, name="x2")
-                nc.vector.tensor_copy(x1[:], dx[k][:].indirect(pos1_t[:, entries]))
-                nc.vector.tensor_copy(x2[:], dx[k][:].indirect(pos2_t[:, entries]))
-                y = fin.tile([P, width], F32, name="y")
-                nc.vector.tensor_tensor(y[:], x1[:], x2[:], ADD)
-                nc.sync.dma_start(out[k * P : (k + 1) * P, j0 : j0 + width], y[:])
+        def fetch(k, j0, width):
+            entries = slice(j0 // 16, (j0 + width) // 16)
+            x1 = fin.tile([P, width], F32, name="x1")
+            x2 = fin.tile([P, width], F32, name="x2")
+            nc.vector.tensor_copy(x1[:], dx[k][:].indirect(pos1_t[:, entries]))
+            nc.vector.tensor_copy(x2[:], dx[k][:].indirect(pos2_t[:, entries]))
+            return x1, x2
+
+        def combine(k, j0, width, x1, x2):
+            y = fin.tile([P, width], F32, name="y")
+            nc.vector.tensor_tensor(y[:], x1[:], x2[:], ADD)
+            nc.sync.dma_start(out[k * P : (k + 1) * P, j0 : j0 + width], y[:])
+
+        pieces = [(0, 0, 512), (0, 512, 512), (1, 0, 512), (1, 512, 256), (1, 768, 256)]
+        fetched = [fetch(*pieces[0])]
+        for i in range(len(pieces)):
+            if i + 1 < len(pieces):
+                fetched.append(fetch(*pieces[i + 1]))
+            combine(*pieces[i], *fetched[i])

from contextlib import ExitStack

import concourse.mybir as mybir

K, T, E, C, H, N = 256, 1024, 8, 256, 512, 512
S = E * C
FLOPS = 2 * S * N * H + 2 * (2 * S * H * K)
BYTES = 4 * (N * T + 2 * H * S + S + K * T) + E * (2 * 128 * H + 16 * H + 2 * (2 * 128 * K + 16 * K)) + 2 * 128 * (S + 2 * T) // 16

F32 = mybir.dt.float32
BF16 = mybir.dt.bfloat16
U32 = mybir.dt.uint32
I32 = mybir.dt.int32
U16 = mybir.dt.uint16
U8 = mybir.dt.uint8
FP8X4 = mybir.dt.float8_e4m3fn_x4
FP4X4 = mybir.dt.float4_e2m1fn_x4
ADD, SUB, MULT = mybir.AluOpType.add, mybir.AluOpType.subtract, mybir.AluOpType.mult
IDENT = mybir.ActivationFunctionType.Identity
SILU = mybir.ActivationFunctionType.Silu
TANH = mybir.ActivationFunctionType.Tanh

P = 128
CH = 512
NCH = S // CH
EPC = CH // C
TILE_N = 128
ON_GPSIMD = (2, 3, 4, 5, 6, 7)
AHEAD = 2
LAST_PIECES = ((0, 512), (512, 512))


def tile_moe_bdx_glu_silu_kernel(
    tc, dyT, a1, a3, w2_words, w2_scales, w1_words, w1_scales, w3_words, w3_scales, gate, offs, pos1, pos2, out
):
    nc = tc.nc
    with ExitStack() as ctx:
        pool = lambda name, bufs: ctx.enter_context(tc.tile_pool(name=name, bufs=bufs))
        lists = pool("lists", 1)
        keep = pool("keep", 1)
        raw = pool("raw", 2)
        saved = pool("saved", 2)
        zpool = pool("zpool", 3)
        factors = pool("factors", 5)
        gathered = pool("gathered", 2)
        grad = pool("grad", 4)
        deriv = pool("deriv", 2)
        fin = pool("fin", 2)
        psum_h = ctx.enter_context(tc.psum_pool(name="psum_h", bufs=5))
        psum_x = ctx.enter_context(tc.psum_pool(name="psum_x", bufs=3))

        offs_t = lists.tile([P, S // 16], U16, name="offs_t")
        pos1_t = lists.tile([P, T // 16], U16, name="pos1_t")
        pos2_t = lists.tile([P, T // 16], U16, name="pos2_t")
        dy = [keep.tile([P, T], F32, name=f"dy{t}") for t in range(4)]
        gates = [keep.tile([P, CH], F32, name=f"gates{c}") for c in range(NCH)]
        w2_sraw = keep.tile([P, E, H], U8, name="w2_sraw", align_bytes=64)
        w2 = keep.tile([P, E, 2 * H], U8, name="w2", align_bytes=64)
        w2_s = keep.tile([P, E, H], U8, name="w2_s", align_bytes=64)
        w1 = keep.tile([P, E, 2 * K], U8, name="w1", align_bytes=64)
        w1_s = keep.tile([P, E, K], U8, name="w1_s", align_bytes=64)
        w3 = keep.tile([P, E, 2 * K], U8, name="w3", align_bytes=64)
        w3_s = keep.tile([P, E, K], U8, name="w3_s", align_bytes=64)
        dx = [keep.tile([P, S], F32, name=f"dx{k}") for k in range(2)]

        for plane in (w2_sraw, w1_s, w3_s):
            nc.gpsimd.memset(plane[:].bitcast(I32), 0)

        def load_scales(plane, scales):
            rows = scales.bitcast(I32).rearrange("e s f i -> f (e s) i")
            for q in range(4):
                nc.sync.dma_start(plane[32 * q : 32 * q + 4, :, :].bitcast(I32), rows[4 * q : 4 * q + 4])

        dy_rows = dyT.rearrange("(p t) n -> p t n", t=4)
        a1_rows = a1.rearrange("(p r) s -> p r s", r=4)
        a3_rows = a3.rearrange("(p r) s -> p r s", r=4)
        w2_raw, a1_t, a3_t = {}, {}, {}

        def load_dy(t):
            nc.sync.dma_start(dy[t][:], dy_rows[:, t, :])

        def load_gate(c):
            nc.sync.dma_start(gates[c][:], gate[0:P, c * CH : (c + 1) * CH])

        def load_words(tile, words, es):
            nc.sync.dma_start(tile.bitcast(I32), words.bitcast(I32).rearrange("e s p b -> p (e s) b")[:, es, :])

        def load_w2(c):
            w2_c = raw.tile([P, EPC, 2 * H], U8, name="w2_c", align_bytes=64)
            load_words(w2_c[:], w2_words, slice(c * EPC, (c + 1) * EPC))
            w2_raw[c] = w2_c

        def new_saved(c):
            a1_c = saved.tile([P, 4, CH], F32, name="a1_c")
            a3_c = saved.tile([P, 4, CH], F32, name="a3_c")
            a1_t[c], a3_t[c] = a1_c, a3_c

        def load_saved(tile, rows, c, j0=0, width=CH):
            nc.sync.dma_start(tile[:, :, j0 : j0 + width], rows[:, :, c * CH + j0 : c * CH + j0 + width])

        new_saved(0)
        nc.sync.dma_start(offs_t[:], offs)
        load_dy(0)
        load_gate(0)
        load_dy(1)
        load_dy(2)
        load_saved(a1_t[0], a1_rows, 0, 0, C)
        load_dy(3)
        load_gate(1)
        load_w2(0)
        load_scales(w2_sraw, w2_scales)
        load_saved(a1_t[0], a1_rows, 0, C, C)
        load_gate(2)
        load_saved(a3_t[0], a3_rows, 0)
        load_w2(1)
        load_gate(3)
        new_saved(1)
        load_saved(a1_t[1], a1_rows, 1)
        load_words(w1[:], w1_words, slice(0, E))
        load_words(w3[:], w3_words, slice(0, E))
        load_scales(w1_s, w1_scales)
        load_scales(w3_s, w3_scales)
        load_saved(a3_t[1], a3_rows, 1)

        def permute_w2(c):
            es = slice(c * EPC, (c + 1) * EPC)
            nc.vector.tensor_copy(
                out=w2[:, es, :].bitcast(U16).rearrange("p e (r m) -> p e r m", r=4),
                in_=w2_raw[c][:].bitcast(U16).rearrange("p e (m r) -> p e r m", r=4),
            )
            nc.vector.tensor_copy(
                out=w2_s[:, es, :].rearrange("p e (r m) -> p e r m", r=4),
                in_=w2_sraw[:, es, :].rearrange("p e (m r) -> p e r m", r=4),
            )

        g16, gq, gs = {}, {}, {}

        def gather(c):
            g32 = gathered.tile([P, 4, CH], F32, name="g32")
            for t in range(4):
                nc.vector.tensor_tensor(
                    g32[:, t, :],
                    dy[t][:].indirect(offs_t[:, c * CH // 16 : (c + 1) * CH // 16]),
                    gates[c][:],
                    MULT,
                )
            g16_c = grad.tile([P, CH, 4], BF16, name="g16_c", align_bytes=64)
            nc.scalar.copy(
                g16_c[:].rearrange("p (c i) t -> p c t i", i=4), g32[:].rearrange("p t (c i) -> p c t i", i=4)
            )
            g16[c] = g16_c

        def quantize_g(c):
            gq_c = grad.tile([P, CH], U32, name="gq_c", align_bytes=64)
            gs_c = grad.tile([P, CH], U8, name="gs_c", align_bytes=64)
            nc.vector.quantize_mx(
                out=gq_c[:].bitcast(FP8X4), scales=gs_c[:], in_=g16[c][:].rearrange("p n t -> p (n t)")
            )
            gq[c], gs[c] = gq_c, gs_c

        ms, zs = {}, {}

        def scalar_part(e):
            zn = zpool.tile([P, 4, C], F32, name="zn")
            ms_e = factors.tile([P, 2, 4, C], F32, name="ms_e")
            mine = a1_t[e // EPC][:, :, (e % EPC) * C : (e % EPC + 1) * C]
            nc.scalar.activation(zn[:], mine, SILU, scale=-1.0)
            nc.scalar.activation(ms_e[:, 0], mine, TANH, scale=0.5)
            nc.scalar.activation(ms_e[:, 0], ms_e[:, 0], IDENT, scale=-0.5, bias=-0.5)
            nc.scalar.activation(ms_e[:, 1], mine, SILU)
            ms[e], zs[e] = ms_e, zn

        def times_a3(e):
            mine = a3_t[e // EPC][:, :, (e % EPC) * C : (e % EPC + 1) * C]
            nc.vector.scalar_tensor_tensor(zs[e][:], zs[e][:], 1.0, mine, SUB, MULT)

        def times_r(e):
            engine = nc.gpsimd if e in ON_GPSIMD else nc.vector
            engine.tensor_tensor(ms[e][:, 0], zs[e][:], ms[e][:, 0], MULT)

        da, da_q, acc = {}, {}, {}

        def new_da(e):
            da_e = deriv.tile([P, 2, 2, TILE_N, 4], BF16, name="da_e", align_bytes=64)
            dq_e = deriv.tile([P, 2, 2, TILE_N], U32, name="dq_e", align_bytes=64)
            ds_e = deriv.tile([P, 2, 2, TILE_N], U8, name="ds_e", align_bytes=64)
            acc_e = psum_x.tile([P, 2, C], F32, name="acc_e")
            da[e], da_q[e], acc[e] = da_e, (dq_e, ds_e), acc_e

        def multiply_dh(e, halves):
            for h in halves:
                slots = slice((e % EPC) * C + h * TILE_N, (e % EPC) * C + (h + 1) * TILE_N)
                dh = psum_h.tile([P, 4, TILE_N], F32, name="dh")
                for r in range(4):
                    nc.tensor.matmul_mx(
                        out=dh[:, r, :],
                        lhsT=w2[:, e, r * 2 * P : (r + 1) * 2 * P].bitcast(FP4X4),
                        lhsT_scale=w2_s[:, e, r * P : (r + 1) * P],
                        rhs=gq[e // EPC][:, slots].bitcast(FP8X4),
                        rhs_scale=gs[e // EPC][:, slots],
                        start=True,
                        stop=True,
                    )
                for x in range(2):
                    nc.vector.tensor_tensor(
                        da[e][:, h, x].rearrange("p (c i) r -> p c r i", i=4),
                        ms[e][:, x, :, h * TILE_N : (h + 1) * TILE_N].rearrange("p r (c i) -> p c r i", i=4),
                        dh[:].rearrange("p r (c i) -> p c r i", i=4),
                        MULT,
                    )

        def finish(e, halves):
            dq, ds = da_q[e]
            hs = slice(halves[0], halves[-1] + 1)
            nc.vector.quantize_mx(
                out=dq[:, hs].rearrange("p h x n -> p (h x n)").bitcast(FP8X4),
                scales=ds[:, hs].rearrange("p h x n -> p (h x n)"),
                in_=da[e][:, hs].rearrange("p h x n r -> p (h x n r)"),
            )
            c0, c1 = hs.start * TILE_N, hs.stop * TILE_N
            for k in range(2):
                for h in halves:
                    for x, w, w_s in ((0, w1, w1_s), (1, w3, w3_s)):
                        nc.tensor.matmul_mx(
                            out=acc[e][:, k, h * TILE_N : (h + 1) * TILE_N],
                            lhsT=w[:, e, k * 2 * P : (k + 1) * 2 * P].bitcast(FP4X4),
                            lhsT_scale=w_s[:, e, k * P : (k + 1) * P],
                            rhs=dq[:, h, x].bitcast(FP8X4),
                            rhs_scale=ds[:, h, x],
                            start=(x == 0),
                            stop=(x == 1),
                        )
                nc.scalar.copy(dx[k][:, e * C + c0 : e * C + c1], acc[e][:, k, c0:c1])

        for c in range(NCH):
            gather(c)
            if c >= 1:
                quantize_g(c - 1)
                permute_w2(c - 1)
                if c + 1 < NCH:
                    load_w2(c + 1)
        quantize_g(NCH - 1)
        permute_w2(NCH - 1)

        for e in range(AHEAD):
            scalar_part(e)
        for e in range(AHEAD):
            times_a3(e)
        for e in range(AHEAD):
            times_r(e)
        for e in range(E):
            ahead = e + AHEAD
            if ahead < E:
                if ahead % EPC == 0 and ahead // EPC + 1 < NCH and ahead // EPC + 1 >= 2:
                    c = ahead // EPC + 1
                    new_saved(c)
                    load_saved(a1_t[c], a1_rows, c)
                    load_saved(a3_t[c], a3_rows, c)
                scalar_part(ahead)
            if e == 3:
                nc.sync.dma_start(pos1_t[:], pos1)
                nc.sync.dma_start(pos2_t[:], pos2)
            if ahead < E:
                times_a3(ahead)
                times_r(ahead)
            new_da(e)
            if e == E - 1:
                finish(e - 1, (0, 1))
                for h in range(2):
                    multiply_dh(e, (h,))
                    finish(e, (h,))
            else:
                multiply_dh(e, (0, 1))
                if e > 0:
                    finish(e - 1, (0, 1))

        def fetch(k, j0, width):
            entries = slice(j0 // 16, (j0 + width) // 16)
            x1 = fin.tile([P, width], F32, name="x1")
            x2 = fin.tile([P, width], F32, name="x2")
            nc.vector.tensor_copy(x1[:], dx[k][:].indirect(pos1_t[:, entries]))
            nc.vector.tensor_copy(x2[:], dx[k][:].indirect(pos2_t[:, entries]))
            return x1, x2

        def combine(k, j0, width, x1, x2):
            y = fin.tile([P, width], F32, name="y")
            nc.vector.tensor_tensor(y[:], x1[:], x2[:], ADD)
            nc.sync.dma_start(out[k * P : (k + 1) * P, j0 : j0 + width], y[:])

        pieces = [(0, 0, 512), (0, 512, 512), (1, 0, 512), (1, 512, 256), (1, 768, 256)]
        fetched = [fetch(*pieces[0])]
        for i in range(len(pieces)):
            if i + 1 < len(pieces):
                fetched.append(fetch(*pieces[i + 1]))
            combine(*pieces[i], *fetched[i])
